import numpy as np
import ml_dtypes


def mxq(x, axis, fmt="e4m3"):
    dtype, down = {"e4m3": (ml_dtypes.float8_e4m3fn, 7), "e5m2": (ml_dtypes.float8_e5m2, 14)}[fmt]
    v = np.moveaxis(np.asarray(x, np.float32).astype(ml_dtypes.bfloat16).astype(np.float64), axis, -1)
    blocks = v.reshape(v.shape[:-1] + (-1, 32))
    amax = np.abs(blocks).max(-1, keepdims=True)
    byte = np.maximum(np.where(amax > 0, np.frexp(amax)[1] - 1 + 127, 0) - down, 1)
    scale = np.exp2(byte - 127.0)
    codes = (blocks / scale).astype(np.float32).astype(dtype).astype(np.float64)
    return np.moveaxis((codes * scale).reshape(v.shape), -1, axis)


WIDE = False


def mx_kscale(k):
    if not WIDE:
        return np.ones(k)
    levels = np.array([10, -10, 5, -5, 0])
    if k % 512:
        return np.exp2(np.random.permutation(np.resize(levels, k // 32))).repeat(32)
    a = np.empty((k // 512, 16))
    for p in range(k // 512):
        a[p, :8] = np.random.permutation(np.resize(levels, 8))
        for g in range(8):
            far = levels[np.abs(levels - a[p, g]) >= 10]
            a[p, g + 8] = far[np.random.randint(len(far))]
    return np.exp2(a.ravel()).repeat(32)


def f64(x):
    return np.asarray(x).astype(np.float64)


def striped(idx):
    return np.tile(idx.reshape(-1, 16).T, (8, 1)).astype(np.uint16)


def unstriped(offs):
    return offs[:16].T.reshape(-1).astype(np.int64)


def striped8(idx):
    return np.concatenate([x.reshape(-1, 16).T for x in idx]).astype(np.uint16)


def runs(offs, k):
    lists = np.stack([offs[16 * r : 16 * r + 16].T.reshape(-1) for r in range(8)]).astype(np.int64)
    return lists[np.arange(k) % 512 // 64]


def pack_weight(w):
    k, n = w.shape
    w = f64(np.asarray(w, np.float32).astype(ml_dtypes.bfloat16)).reshape(k // 32, 32, n)
    amax = np.abs(w).max(1)
    byte = np.clip(np.where(amax > 0, np.frexp(amax)[1] - 1 + 127 - 7, 1), 1, 254)
    scaled = (w * np.exp2(127.0 - byte)[:, None, :]).reshape(k, n).astype(np.float32)
    words = np.ascontiguousarray(scaled.reshape(k // 512, 128, 4, n).transpose(0, 1, 3, 2)).astype(ml_dtypes.float8_e4m3fn).view(np.uint8)
    return words, np.ascontiguousarray(byte.astype(np.uint8).reshape(k // 512, 16, n))


def unpack_weight(words, scales):
    g, p, n, _ = words.shape
    vals = np.ascontiguousarray(words).view(ml_dtypes.float8_e4m3fn).astype(np.float64) * np.repeat(np.exp2(scales.astype(np.float64) - 127.0), 8, axis=1)[..., None]
    return vals.transpose(0, 1, 3, 2).reshape(g * 512, n)


def sigmoid(v):
    return 1.0 / (1.0 + np.exp(-np.maximum(v, -700.0)))

def planes(y):
    n, m = y.shape
    v = y.astype(np.float32).astype(ml_dtypes.bfloat16).astype(np.float64).reshape(n // 32, 32, m)
    top = np.abs(v).max(1)
    byte = np.clip(np.where(top > 0, np.frexp(top)[1] - 1 + 127 - 7, 1), 1, 254)
    codes = (v * np.exp2(127.0 - byte)[:, None, :]).reshape(n, m).astype(np.float32).astype(ml_dtypes.float8_e4m3fn).view(np.uint8)
    words = codes.reshape(n // 512, 128, 4, m).transpose(0, 1, 3, 2)
    return np.ascontiguousarray(words), np.ascontiguousarray(byte.astype(np.uint8).reshape(n // 512, 16, m))


K, T, S, V, H = 512, 2048, 512, 512, 512


def setup_inputs():
    n = np.random.standard_normal
    s = mx_kscale(K)[:, None]
    u = mx_kscale(S)
    packed_xT = pack_weight(n((K, T)) * s)
    packed_w1 = pack_weight(n((K, H)) / np.sqrt(K) / s)
    packed_w2 = pack_weight(n((K, H)) / np.sqrt(K) / s)
    return {
        "x_words": packed_xT[0],
        "x_scales": packed_xT[1],
        "w1_words": packed_w1[0],
        "w1_scales": packed_w1[1],
        "w2_words": packed_w2[0],
        "w2_scales": packed_w2[1],
        "ga": (np.random.uniform(0.5, 1.5, (H, 1)) * u[:, None]).astype(np.float32),
        "gb": (np.random.uniform(0.5, 1.5, (H, 1)) / u[:, None]).astype(np.float32),
        "offs": striped(np.random.permutation(T)[:S]),
        "two": striped(np.random.permutation(T)[:V]),
        "n1": striped8(np.stack([np.random.permutation(S) for _ in range(8)])),
        "n2": striped8(np.stack([np.random.permutation(S) for _ in range(8)])),
        "n3": striped8(np.stack([np.random.permutation(V) for _ in range(8)])),
        "n4": striped8(np.stack([np.random.permutation(V) for _ in range(8)])),
        "n5": striped8(np.stack([np.random.permutation(V) for _ in range(8)])),
        "n6": striped8(np.stack([np.random.permutation(V) for _ in range(8)])),
    }


def reference(x_words, x_scales, w1_words, w1_scales, w2_words, w2_scales, ga, gb, offs, two, n1, n2, n3, n4, n5, n6):
    xq = unpack_weight(x_words, x_scales)[:, unstriped(offs)]
    a = unpack_weight(w1_words, w1_scales).T @ xq
    pa = a[np.arange(H)[:, None], runs(n1, H)]
    pb = a[np.arange(H)[:, None], runs(n2, H)]
    z = f64(ga) * (np.maximum(np.minimum(a, pa), np.minimum(np.maximum(a, pa), pb)))
    x_two = unpack_weight(x_words, x_scales)[:, unstriped(two)]
    b = unpack_weight(w2_words, w2_scales).T @ x_two
    st = b[np.arange(H)[:, None], runs(n3, H)] - b
    z2 = f64(gb) * (b * (sigmoid(st[np.arange(H)[:, None], runs(n4, H)])))
    s = 0.0625 * ((mxq(z, 0, "e4m3").T @ mxq(z2, 0, "e4m3")))
    st2 = s + 0.5 * (s[np.arange(S)[:, None], runs(n5, S)])
    out_0 = st2 - (st2[np.arange(S)[:, None], runs(n6, S)])
    return (out_0,) + planes(out_0)

@@ -1,0 +1,191 @@
+from contextlib import ExitStack
+
+import concourse.mybir as mybir
+
+F32 = mybir.dt.float32
+BF16 = mybir.dt.bfloat16
+I32 = mybir.dt.int32
+U32 = mybir.dt.uint32
+U16 = mybir.dt.uint16
+U8 = mybir.dt.uint8
+FP8X4 = mybir.dt.float8_e4m3fn_x4
+ALU = mybir.AluOpType
+ACT = mybir.ActivationFunctionType
+
+P = 128
+PACK = 4
+T = 2048
+N = 512
+WIDE = 2 * N
+FLOPS = 3 * 2 * 512 * 512 * 512
+OUT_CHUNKS = ((0, 256), (256, 128), (384, 128))
+
+
+def tile_picked_kqmedhopdhop_none_po_kernel(tc, x_words, x_scales, w1_words, w1_scales, w2_words, w2_scales, ga, gb,
+        offs, two, n1, n2, n3, n4, n5, n6, out_0, out_1, out_2):
+    nc = tc.nc
+    with ExitStack() as ctx:
+        lists = ctx.enter_context(tc.tile_pool(name="lists", bufs=1))
+        sb = ctx.enter_context(tc.tile_pool(name="sb", bufs=1))
+        psum = ctx.enter_context(tc.psum_pool(name="psum", bufs=1))
+
+        def tile(name, shape, dtype):
+            return sb.tile(shape, dtype, name=name, align_bytes=64)
+
+        def load_list(name, src):
+            held = lists.tile([P, N // 16], U16, name=name)
+            nc.sync.dma_start(held[:], src)
+            return held
+
+        def load_words(name, src, width):
+            held = tile(name, [P, width], I32)
+            nc.sync.dma_start(held[:], src[0].rearrange("p n t -> p (n t)").bitcast(I32))
+            return held
+
+        def load_scales(name, src, width, queue):
+            held = tile(name, [P, width], U8)
+            nc.vector.memset(held[:].bitcast(I32), 0)
+            for q in range(4):
+                queue.dma_start(held[32 * q : 32 * q + 4, :].bitcast(I32), src[0, 4 * q : 4 * q + 4, :].bitcast(I32))
+            return held
+
+        def load_gain(name, src):
+            held = tile(name, [P, PACK], F32)
+            nc.sync.dma_start(held[:], src.rearrange("(p t) o -> p (t o)", t=PACK))
+            return held
+
+        two_l = load_list("two_l", two)
+        xs = load_scales("xs", x_scales, T, nc.scalar)
+        warm = tile("warm", [P, 2], F32)
+        nc.vector.memset(warm[:, 0:1], 0.0)
+        nc.scalar.activation(warm[:, 1:2], warm[:, 0:1], ACT.Sigmoid)
+
+        xw = load_words("xw", x_words, T)
+        w2w = load_words("w2w", w2_words, N)
+        offs_l = load_list("offs_l", offs)
+        w2s = load_scales("w2s", w2_scales, N, nc.sync)
+        w1w = load_words("w1w", w1_words, N)
+        w1s = load_scales("w1s", w1_scales, N, nc.gpsimd)
+        n3_l = load_list("n3_l", n3)
+        ga_t = load_gain("ga_t", ga)
+        n1_l = load_list("n1_l", n1)
+        n2_l = load_list("n2_l", n2)
+        n4_l = load_list("n4_l", n4)
+        gb_t = load_gain("gb_t", gb)
+        n5_l = load_list("n5_l", n5)
+        n6_l = load_list("n6_l", n6)
+
+        def pick_scales(name, picks):
+            got = tile(name, [P, N], U8)
+            nc.vector.tensor_copy(got[:], xs[:].indirect(picks[:]))
+            return got
+
+        def pick_words(name, picks):
+            got = tile(name, [P, N], I32)
+            nc.vector.tensor_copy(got[:].bitcast(U32), xw[:].bitcast(U32).indirect(picks[:]))
+            return got
+
+        def deal(name, src, dtype):
+            dealt = tile(name, [P, PACK, P], dtype)
+            nc.vector.tensor_copy(dealt[:].rearrange("p t m -> p m t"), src[:].rearrange("p (m t) -> p m t", t=PACK))
+            return dealt
+
+        def product(tag, t, lw, ls, rw, rs):
+            bank = psum.tile([P, N], F32, name=f"{tag}{t}", tag=f"{tag}{t}")
+            nc.tensor.matmul_mx(out=bank[:], lhsT=lw.bitcast(FP8X4), lhsT_scale=ls, rhs=rw.bitcast(FP8X4), rhs_scale=rs, start=True, stop=True)
+            return bank
+
+        xs_two = pick_scales("xs_two", two_l)
+        w2wd = deal("w2wd", w2w, I32)
+        xs_offs = pick_scales("xs_offs", offs_l)
+        w2sd = deal("w2sd", w2s, U8)
+        xw_two = pick_words("xw_two", two_l)
+        xw_offs = pick_words("xw_offs", offs_l)
+        w1wd = deal("w1wd", w1w, I32)
+        w1sd = deal("w1sd", w1s, U8)
+
+        b_plain = tile("b_plain", [P, PACK, N], F32)
+        st_win = []
+        for t in range(PACK):
+            bank = product("pb", t, w2wd[:, t, :], w2sd[:, t, :], xw_two[:], xs_two[:])
+            b_win = tile(f"b_win{t}", [P, WIDE], F32)
+            nc.scalar.copy(b_win[:, 0:N], bank[:])
+            nc.scalar.copy(b_plain[:, t, :], bank[:])
+            st = tile(f"st_win{t}", [P, WIDE], F32)
+            nc.vector.tensor_tensor(st[:, 0:N], b_win[:].indirect(n3_l[:]), b_plain[:, t, :], ALU.subtract)
+            st_win.append(st)
+
+        a_win = []
+        for t in range(PACK):
+            bank = product("pa", t, w1wd[:, t, :], w1sd[:, t, :], xw_offs[:], xs_offs[:])
+            win = tile(f"a_win{t}", [P, WIDE], F32)
+            nc.scalar.activation(win[:, 0:N], bank[:], ACT.Copy, scale=ga_t[:, t : t + 1])
+            a_win.append(win)
+
+        z2 = tile("z2", [P, PACK, N], F32)
+        for t in range(PACK):
+            nc.scalar.activation(z2[:, t, :], st_win[t][:].indirect(n4_l[:]), ACT.Sigmoid)
+
+        pa = tile("pa", [P, PACK, N], F32)
+        pb = tile("pb", [P, PACK, N], F32)
+        lo = tile("lo", [P, PACK, N], F32)
+        hi = tile("hi", [P, PACK, N], F32)
+        for t in range(PACK):
+            nc.vector.tensor_copy(pa[:, t, :], a_win[t][:].indirect(n1_l[:]))
+            nc.vector.tensor_copy(pb[:, t, :], a_win[t][:].indirect(n2_l[:]))
+            nc.vector.tensor_tensor(lo[:, t, :], a_win[t][:, 0:N], pa[:, t, :], ALU.min)
+            nc.vector.tensor_tensor(hi[:, t, :], a_win[t][:, 0:N], pa[:, t, :], ALU.max)
+
+        for t in range(PACK):
+            nc.vector.scalar_tensor_tensor(z2[:, t, :], b_plain[:, t, :], gb_t[:, t : t + 1], z2[:, t, :], ALU.mult, ALU.mult)
+        z2b = tile("z2b", [P, N, PACK], BF16)
+        nc.scalar.copy(z2b[:].rearrange("p (c i) t -> p c t i", i=4), z2[:].rearrange("p t (c i) -> p c t i", i=4))
+
+        zb = tile("zb", [P, PACK, P, PACK], BF16)
+        nc.vector.tensor_tensor(hi[:], hi[:], pb[:], ALU.min)
+        z2w = tile("z2w", [P, N], I32)
+        z2s = tile("z2s", [P, N], U8)
+        nc.vector.quantize_mx(out=z2w[:].bitcast(FP8X4), scales=z2s[:], in_=z2b[:].rearrange("p c t -> p (c t)"))
+        for h in range(4):
+            cols = slice(P * h, P * (h + 1))
+            nc.vector.tensor_tensor(lo[:, :, cols], lo[:, :, cols], hi[:, :, cols], ALU.max)
+            nc.scalar.copy(zb[:, :, 32 * h : 32 * (h + 1), :].rearrange("p u m t -> p m t u"),
+                           lo[:, :, cols].rearrange("p t (m u) -> p m t u", u=PACK))
+
+        st2_win = []
+        st2_plain = tile("st2_plain", [P, PACK, N], F32)
+        s_plain = tile("s_plain", [P, PACK, N], F32)
+        banks = []
+        for u in range(PACK):
+            zw = tile(f"zw{u}", [P, P], I32)
+            zs = tile(f"zs{u}", [P, P], U8)
+            nc.vector.quantize_mx(out=zw[:].bitcast(FP8X4), scales=zs[:], in_=zb[:, u, :, :].rearrange("p m t -> p (m t)"))
+            banks.append(product("pb", u, zw[:], zs[:], z2w[:], z2s[:]))
+        for u in range(PACK):
+            s_win = tile(f"s_win{u}", [P, WIDE], F32)
+            nc.scalar.activation(s_win[:, 0:N], banks[u][:], ACT.Copy, scale=-1.0 / 32.0)
+            nc.scalar.activation(s_plain[:, u, :], banks[u][:], ACT.Copy, scale=-1.0 / 16.0)
+            st2 = tile(f"st2_win{u}", [P, N], F32)
+            nc.vector.tensor_tensor(st2[:], s_win[:].indirect(n5_l[:]), s_plain[:, u, :], ALU.add)
+            st2_win.append(st2)
+        for u in range(PACK):
+            nc.scalar.copy(st2_plain[:, u, :], st2_win[u][:])
+
+        rows = out_0.rearrange("(p t) v -> p t v", t=PACK)
+        words_out = out_1[0].rearrange("p c r -> p (c r)").bitcast(I32)
+        os_t = tile("os_t", [P, N], U8)
+        for h, (c0, width) in enumerate(OUT_CHUNKS):
+            cols = slice(c0, c0 + width)
+            y = tile(f"y{h}", [P, PACK, width], F32)
+            for u in range(PACK):
+                nc.vector.tensor_tensor(y[:, u, :], st2_win[u][:].indirect(n6_l[:, c0 // 16 : (c0 + width) // 16]),
+                                        st2_plain[:, u, cols], ALU.subtract)
+            nc.sync.dma_start(rows[:, :, cols], y[:])
+            yb = tile(f"yb{h}", [P, width, PACK], BF16)
+            nc.scalar.copy(yb[:].rearrange("p (c i) t -> p c t i", i=4), y[:].rearrange("p t (c i) -> p c t i", i=4))
+            yw = tile(f"yw{h}", [P, width], I32)
+            nc.vector.quantize_mx(out=yw[:].bitcast(FP8X4), scales=os_t[:, cols], in_=yb[:].rearrange("p c t -> p (c t)"))
+            nc.sync.dma_start(words_out[:, cols], yw[:])
+        for q in range(4):
+            queue = nc.scalar if q % 2 else nc.sync
+            queue.dma_start(out_2[0, 4 * q : 4 * q + 4, :].bitcast(I32), os_t[32 * q : 32 * q + 4, :].bitcast(I32))

@@ -1,6 +1,7 @@
 from contextlib import ExitStack
 
 import concourse.mybir as mybir
+from concourse.masks import make_identity
 
 F32 = mybir.dt.float32
 BF16 = mybir.dt.bfloat16
@@ -49,29 +50,29 @@ def tile_picked_kqmedhopdhop_none_po_kernel(tc, x_words, x_scales, w1_words, w1_
                 queue.dma_start(held[32 * q : 32 * q + 4, :].bitcast(I32), src[0, 4 * q : 4 * q + 4, :].bitcast(I32))
             return held
 
-        def load_gain(name, src):
-            held = tile(name, [P, PACK], F32)
-            nc.sync.dma_start(held[:], src.rearrange("(p t) o -> p (t o)", t=PACK))
-            return held
-
         two_l = load_list("two_l", two)
-        xs = load_scales("xs", x_scales, T, nc.scalar)
+        xw = load_words("xw", x_words, T)
+        xs = load_scales("xs", x_scales, T, nc.sync)
+        w2w = load_words("w2w", w2_words, N)
+        offs_l = load_list("offs_l", offs)
+        w2s = load_scales("w2s", w2_scales, N, nc.scalar)
         warm = tile("warm", [P, 2], F32)
         nc.vector.memset(warm[:, 0:1], 0.0)
         nc.scalar.activation(warm[:, 1:2], warm[:, 0:1], ACT.Sigmoid)
-
-        xw = load_words("xw", x_words, T)
-        w2w = load_words("w2w", w2_words, N)
-        offs_l = load_list("offs_l", offs)
-        w2s = load_scales("w2s", w2_scales, N, nc.sync)
         w1w = load_words("w1w", w1_words, N)
-        w1s = load_scales("w1s", w1_scales, N, nc.gpsimd)
+        w1s = load_scales("w1s", w1_scales, N, nc.sync)
         n3_l = load_list("n3_l", n3)
-        ga_t = load_gain("ga_t", ga)
+
+        gain_rows = tile("gain_rows", [P, P], F32)
+        nc.vector.memset(gain_rows[:], 0.0)
+        for r, gain in enumerate((ga, gb)):
+            nc.sync.dma_start(gain_rows[PACK * r : PACK * (r + 1), :].rearrange("t (b j) -> t b j", j=8),
+                                gain.rearrange("(b t j) o -> t b (j o)", t=PACK, j=8))
+        ident = tile("ident", [P, P], F32)
+        make_identity(nc, ident[:])
         n1_l = load_list("n1_l", n1)
         n2_l = load_list("n2_l", n2)
         n4_l = load_list("n4_l", n4)
-        gb_t = load_gain("gb_t", gb)
         n5_l = load_list("n5_l", n5)
         n6_l = load_list("n6_l", n6)
 
@@ -86,8 +87,9 @@ def tile_picked_kqmedhopdhop_none_po_kernel(tc, x_words, x_scales, w1_words, w1_
             return got
 
         def deal(name, src, dtype):
-            dealt = tile(name, [P, PACK, P], dtype)
-            nc.vector.tensor_copy(dealt[:].rearrange("p t m -> p m t"), src[:].rearrange("p (m t) -> p m t", t=PACK))
+            dealt = tile(name, [P, N], dtype)
+            nc.vector.tensor_copy(dealt[:].bitcast(I32).rearrange("p (t b j) -> p b t j", t=PACK, b=16),
+                                  src[:].bitcast(I32).rearrange("p (b t j) -> p b t j", t=PACK, b=16))
             return dealt
 
         def product(tag, t, lw, ls, rw, rs):
@@ -96,10 +98,10 @@ def tile_picked_kqmedhopdhop_none_po_kernel(tc, x_words, x_scales, w1_words, w1_
             return bank
 
         xs_two = pick_scales("xs_two", two_l)
-        w2wd = deal("w2wd", w2w, I32)
-        xs_offs = pick_scales("xs_offs", offs_l)
-        w2sd = deal("w2sd", w2s, U8)
         xw_two = pick_words("xw_two", two_l)
+        w2wd = deal("w2wd", w2w, I32)
+        w2sd = deal("w2sd", w2s, U8)
+        xs_offs = pick_scales("xs_offs", offs_l)
         xw_offs = pick_words("xw_offs", offs_l)
         w1wd = deal("w1wd", w1w, I32)
         w1sd = deal("w1sd", w1s, U8)
@@ -107,7 +109,7 @@ def tile_picked_kqmedhopdhop_none_po_kernel(tc, x_words, x_scales, w1_words, w1_
         b_plain = tile("b_plain", [P, PACK, N], F32)
         st_win = []
         for t in range(PACK):
-            bank = product("pb", t, w2wd[:, t, :], w2sd[:, t, :], xw_two[:], xs_two[:])
+            bank = product("pb", t, w2wd[:, P * t : P * (t + 1)], w2sd[:, P * t : P * (t + 1)], xw_two[:], xs_two[:])
             b_win = tile(f"b_win{t}", [P, WIDE], F32)
             nc.scalar.copy(b_win[:, 0:N], bank[:])
             nc.scalar.copy(b_plain[:, t, :], bank[:])
@@ -115,42 +117,50 @@ def tile_picked_kqmedhopdhop_none_po_kernel(tc, x_words, x_scales, w1_words, w1_
             nc.vector.tensor_tensor(st[:, 0:N], b_win[:].indirect(n3_l[:]), b_plain[:, t, :], ALU.subtract)
             st_win.append(st)
 
+        gain_bank = psum.tile([P, P], F32, name="gain_bank", tag="pa3")
+        nc.tensor.transpose(gain_bank[:], gain_rows[:], ident[:])
+        gains = tile("gains", [P, 2 * PACK], F32)
+        nc.scalar.copy(gains[:], gain_bank[:, 0 : 2 * PACK])
+
         a_win = []
+        a_plain = tile("a_plain", [P, PACK, N], F32)
         for t in range(PACK):
-            bank = product("pa", t, w1wd[:, t, :], w1sd[:, t, :], xw_offs[:], xs_offs[:])
+            bank = product("pa", t, w1wd[:, P * t : P * (t + 1)], w1sd[:, P * t : P * (t + 1)], xw_offs[:], xs_offs[:])
             win = tile(f"a_win{t}", [P, WIDE], F32)
-            nc.scalar.activation(win[:, 0:N], bank[:], ACT.Copy, scale=ga_t[:, t : t + 1])
+            nc.scalar.activation(win[:, 0:N], bank[:], ACT.Copy, scale=gains[:, t : t + 1])
+            nc.scalar.activation(a_plain[:, t, :], bank[:], ACT.Copy, scale=gains[:, t : t + 1])
             a_win.append(win)
 
         z2 = tile("z2", [P, PACK, N], F32)
         for t in range(PACK):
             nc.scalar.activation(z2[:, t, :], st_win[t][:].indirect(n4_l[:]), ACT.Sigmoid)
 
-        pa = tile("pa", [P, PACK, N], F32)
-        pb = tile("pb", [P, PACK, N], F32)
-        lo = tile("lo", [P, PACK, N], F32)
-        hi = tile("hi", [P, PACK, N], F32)
+        d1 = tile("d1", [P, PACK, N], F32)
+        d2 = tile("d2", [P, PACK, N], F32)
         for t in range(PACK):
-            nc.vector.tensor_copy(pa[:, t, :], a_win[t][:].indirect(n1_l[:]))
-            nc.vector.tensor_copy(pb[:, t, :], a_win[t][:].indirect(n2_l[:]))
-            nc.vector.tensor_tensor(lo[:, t, :], a_win[t][:, 0:N], pa[:, t, :], ALU.min)
-            nc.vector.tensor_tensor(hi[:, t, :], a_win[t][:, 0:N], pa[:, t, :], ALU.max)
+            nc.vector.tensor_tensor(d1[:, t, :], a_win[t][:].indirect(n1_l[:]), a_plain[:, t, :], ALU.subtract)
+            nc.vector.tensor_tensor(d2[:, t, :], a_win[t][:].indirect(n2_l[:]), a_plain[:, t, :], ALU.subtract)
 
         for t in range(PACK):
-            nc.vector.scalar_tensor_tensor(z2[:, t, :], b_plain[:, t, :], gb_t[:, t : t + 1], z2[:, t, :], ALU.mult, ALU.mult)
+            nc.vector.scalar_tensor_tensor(z2[:, t, :], b_plain[:, t, :], gains[:, PACK + t : PACK + t + 1], z2[:, t, :], ALU.mult, ALU.mult)
         z2b = tile("z2b", [P, N, PACK], BF16)
         nc.scalar.copy(z2b[:].rearrange("p (c i) t -> p c t i", i=4), z2[:].rearrange("p t (c i) -> p c t i", i=4))
 
         zb = tile("zb", [P, PACK, P, PACK], BF16)
-        nc.vector.tensor_tensor(hi[:], hi[:], pb[:], ALU.min)
+        nc.vector.scalar_tensor_tensor(d2[:], d1[:], 0.0, d2[:], ALU.max, ALU.min)
         z2w = tile("z2w", [P, N], I32)
         z2s = tile("z2s", [P, N], U8)
         nc.vector.quantize_mx(out=z2w[:].bitcast(FP8X4), scales=z2s[:], in_=z2b[:].rearrange("p c t -> p (c t)"))
+        nc.vector.scalar_tensor_tensor(d2[:], d1[:], 0.0, d2[:], ALU.min, ALU.max)
         for h in range(4):
             cols = slice(P * h, P * (h + 1))
-            nc.vector.tensor_tensor(lo[:, :, cols], lo[:, :, cols], hi[:, :, cols], ALU.max)
-            nc.scalar.copy(zb[:, :, 32 * h : 32 * (h + 1), :].rearrange("p u m t -> p m t u"),
-                           lo[:, :, cols].rearrange("p t (m u) -> p m t u", u=PACK))
+            dealt = zb[:, :, 32 * h : 32 * (h + 1), :].rearrange("p u m t -> p m t u")
+            if h < 3:
+                nc.vector.tensor_tensor(d1[:, :, cols], a_plain[:, :, cols], d2[:, :, cols], ALU.add)
+                nc.scalar.copy(dealt, d1[:, :, cols].rearrange("p t (m u) -> p m t u", u=PACK))
+            else:
+                nc.vector.tensor_tensor(dealt, a_plain[:, :, cols].rearrange("p t (m u) -> p m t u", u=PACK),
+                                        d2[:, :, cols].rearrange("p t (m u) -> p m t u", u=PACK), ALU.add)
 
         st2_win = []
         st2_plain = tile("st2_plain", [P, PACK, N], F32)

@@ -141,42 +141,88 @@ def tile_picked_kqmedhopdhop_none_po_kernel(tc, x_words, x_scales, w1_words, w1_
             nc.vector.tensor_tensor(d1[:, t, :], a_win[t][:].indirect(n1_l[:]), a_plain[:, t, :], ALU.subtract)
             nc.vector.tensor_tensor(d2[:, t, :], a_win[t][:].indirect(n2_l[:]), a_plain[:, t, :], ALU.subtract)
 
+        b_gain = tile("b_gain", [P, PACK, N], F32)
         for t in range(PACK):
-            nc.vector.scalar_tensor_tensor(z2[:, t, :], b_plain[:, t, :], gains[:, PACK + t : PACK + t + 1], z2[:, t, :], ALU.mult, ALU.mult)
-        z2b = tile("z2b", [P, N, PACK], BF16)
-        nc.scalar.copy(z2b[:].rearrange("p (c i) t -> p c t i", i=4), z2[:].rearrange("p t (c i) -> p c t i", i=4))
+            nc.scalar.activation(b_gain[:, t, :], b_plain[:, t, :], ACT.Copy, scale=gains[:, PACK + t : PACK + t + 1])
 
-        zb = tile("zb", [P, PACK, P, PACK], BF16)
-        nc.vector.scalar_tensor_tensor(d2[:], d1[:], 0.0, d2[:], ALU.max, ALU.min)
+        zb = tile("zb", [P, N * PACK], BF16)
+        zb_pairs = zb[:].bitcast(F32).rearrange("p (u m w) -> p u m w", u=PACK, w=2)
+
+        turned = [psum.tile([P, PACK, P], F32, name=f"turned{h}", tag=f"pa{h}") for h in range(3)]
+        for h in range(3):
+            for t in range(PACK):
+                nc.tensor.matmul(turned[h][:, t, :], a_plain[:, t, P * h : P * (h + 1)], ident[:], start=(t == 0), stop=False, is_transpose=True)
+
+        def upper_clamp(h):
+            cols = slice(P * h, P * (h + 1))
+            nc.vector.scalar_tensor_tensor(d2[:, :, cols], d1[:, :, cols], 0.0, d2[:, :, cols], ALU.max, ALU.min)
+
+        def finish_z(h):
+            cols = slice(P * h, P * (h + 1))
+            nc.vector.scalar_tensor_tensor(d2[:, :, cols], d1[:, :, cols], 0.0, d2[:, :, cols], ALU.min, ALU.max)
+            if h == 3:
+                nc.vector.tensor_tensor(zb[:].rearrange("p (u m t) -> p m t u", u=PACK, t=PACK)[:, 32 * h : 32 * (h + 1), :, :],
+                                        a_plain[:, :, cols].rearrange("p t (m u) -> p m t u", u=PACK),
+                                        d2[:, :, cols].rearrange("p t (m u) -> p m t u", u=PACK), ALU.add)
+                return None
+            for t in range(PACK):
+                nc.tensor.matmul(turned[h][:, t, :], d2[:, t, cols], ident[:], start=False, stop=(t == PACK - 1), is_transpose=True)
+            zt = tile(f"zt{h}", [P, N], BF16)
+            nc.scalar.copy(zt[:].rearrange("c (w p e) -> c w p e", w=2, e=2), turned[h][:].rearrange("c (w e) p -> c w p e", e=2))
+            return zt
+
+        def turn_back(h, zt):
+            back = psum.tile([P, 2, P], F32, name=f"back{h}", tag=f"pa{h + 1}")
+            for w in range(2):
+                nc.tensor.transpose(back[:, w, :], zt[:].bitcast(F32)[:, P * w : P * (w + 1)], ident[:])
+            nc.scalar.copy(zb_pairs[:, :, 32 * h : 32 * (h + 1), :], back[:].rearrange("p w (m u) -> p u m w", u=PACK))
+
+        zts = []
+        upper_clamp(0)
+        for h in range(4):
+            if h < 3:
+                upper_clamp(h + 1)
+            zts.append(finish_z(h))
+            if h > 0:
+                turn_back(h - 1, zts[h - 1])
+
+        z2b = tile("z2b", [P, N, PACK], BF16)
         z2w = tile("z2w", [P, N], I32)
         z2s = tile("z2s", [P, N], U8)
-        nc.vector.quantize_mx(out=z2w[:].bitcast(FP8X4), scales=z2s[:], in_=z2b[:].rearrange("p c t -> p (c t)"))
-        nc.vector.scalar_tensor_tensor(d2[:], d1[:], 0.0, d2[:], ALU.min, ALU.max)
-        for h in range(4):
-            cols = slice(P * h, P * (h + 1))
-            dealt = zb[:, :, 32 * h : 32 * (h + 1), :].rearrange("p u m t -> p m t u")
-            if h < 3:
-                nc.vector.tensor_tensor(d1[:, :, cols], a_plain[:, :, cols], d2[:, :, cols], ALU.add)
-                nc.scalar.copy(dealt, d1[:, :, cols].rearrange("p t (m u) -> p m t u", u=PACK))
-            else:
-                nc.vector.tensor_tensor(dealt, a_plain[:, :, cols].rearrange("p t (m u) -> p m t u", u=PACK),
-                                        d2[:, :, cols].rearrange("p t (m u) -> p m t u", u=PACK), ALU.add)
+        halves = (slice(0, N // 2), slice(N // 2, N))
+        for cols in halves:
+            nc.vector.tensor_tensor(z2b[:, cols, :].rearrange("p (c i) t -> p c t i", i=4),
+                                    b_gain[:, :, cols].rearrange("p t (c i) -> p c t i", i=4),
+                                    z2[:, :, cols].rearrange("p t (c i) -> p c t i", i=4), ALU.mult)
+        for cols in halves:
+            nc.vector.quantize_mx(out=z2w[:, cols].bitcast(FP8X4), scales=z2s[:, cols], in_=z2b[:, cols, :].rearrange("p c t -> p (c t)"))
 
         st2_win = []
         st2_plain = tile("st2_plain", [P, PACK, N], F32)
         s_plain = tile("s_plain", [P, PACK, N], F32)
-        banks = []
+        s_win = [tile(f"s_win{u}", [P, WIDE], F32) for u in range(PACK)]
+        zq = []
         for u in range(PACK):
             zw = tile(f"zw{u}", [P, P], I32)
             zs = tile(f"zs{u}", [P, P], U8)
-            nc.vector.quantize_mx(out=zw[:].bitcast(FP8X4), scales=zs[:], in_=zb[:, u, :, :].rearrange("p m t -> p (m t)"))
-            banks.append(product("pb", u, zw[:], zs[:], z2w[:], z2s[:]))
+            nc.vector.quantize_mx(out=zw[:].bitcast(FP8X4), scales=zs[:], in_=zb[:, N * u : N * (u + 1)])
+            zq.append((zw, zs))
+        first = []
+        for tag, cols in zip(("pa0", "pb0"), halves):
+            bank = psum.tile([P, N // 2], F32, name=f"first_{tag}", tag=tag)
+            nc.tensor.matmul_mx(out=bank[:], lhsT=zq[0][0][:].bitcast(FP8X4), lhsT_scale=zq[0][1][:],
+                                rhs=z2w[:, cols].bitcast(FP8X4), rhs_scale=z2s[:, cols], start=True, stop=True)
+            first.append(bank)
+        banks = [product("pb", u, zq[u][0][:], zq[u][1][:], z2w[:], z2s[:]) for u in range(1, PACK)]
+        nc.scalar.activation(s_win[0][:, halves[0]], first[0][:], ACT.Copy, scale=-1.0 / 32.0)
+        nc.vector.tensor_scalar(s_win[0][:, halves[1]], first[1][:], -1.0 / 32.0, None, ALU.mult)
+        nc.vector.tensor_scalar(s_plain[:, 0, :], s_win[0][:, 0:N], 2.0, None, ALU.mult)
         for u in range(PACK):
-            s_win = tile(f"s_win{u}", [P, WIDE], F32)
-            nc.scalar.activation(s_win[:, 0:N], banks[u][:], ACT.Copy, scale=-1.0 / 32.0)
-            nc.scalar.activation(s_plain[:, u, :], banks[u][:], ACT.Copy, scale=-1.0 / 16.0)
+            if u > 0:
+                nc.scalar.activation(s_win[u][:, 0:N], banks[u - 1][:], ACT.Copy, scale=-1.0 / 32.0)
+                nc.scalar.activation(s_plain[:, u, :], banks[u - 1][:], ACT.Copy, scale=-1.0 / 16.0)
             st2 = tile(f"st2_win{u}", [P, N], F32)
-            nc.vector.tensor_tensor(st2[:], s_win[:].indirect(n5_l[:]), s_plain[:, u, :], ALU.add)
+            nc.vector.tensor_tensor(st2[:], s_win[u][:].indirect(n5_l[:]), s_plain[:, u, :], ALU.add)
             st2_win.append(st2)
         for u in range(PACK):
             nc.scalar.copy(st2_plain[:, u, :], st2_win[u][:])
@@ -192,7 +238,8 @@ def tile_picked_kqmedhopdhop_none_po_kernel(tc, x_words, x_scales, w1_words, w1_
                                         st2_plain[:, u, cols], ALU.subtract)
             nc.sync.dma_start(rows[:, :, cols], y[:])
             yb = tile(f"yb{h}", [P, width, PACK], BF16)
-            nc.scalar.copy(yb[:].rearrange("p (c i) t -> p c t i", i=4), y[:].rearrange("p t (c i) -> p c t i", i=4))
+            rounding_copy = nc.vector.tensor_copy if h == len(OUT_CHUNKS) - 1 else nc.scalar.copy
+            rounding_copy(yb[:].rearrange("p (c i) t -> p c t i", i=4), y[:].rearrange("p t (c i) -> p c t i", i=4))
             yw = tile(f"yw{h}", [P, width], I32)
             nc.vector.quantize_mx(out=yw[:].bitcast(FP8X4), scales=os_t[:, cols], in_=yb[:].rearrange("p c t -> p (c t)"))
             nc.sync.dma_start(words_out[:, cols], yw[:])

@@ -56,9 +56,6 @@ def tile_picked_kqmedhopdhop_none_po_kernel(tc, x_words, x_scales, w1_words, w1_
         w2w = load_words("w2w", w2_words, N)
         offs_l = load_list("offs_l", offs)
         w2s = load_scales("w2s", w2_scales, N, nc.scalar)
-        warm = tile("warm", [P, 2], F32)
-        nc.vector.memset(warm[:, 0:1], 0.0)
-        nc.scalar.activation(warm[:, 1:2], warm[:, 0:1], ACT.Sigmoid)
         w1w = load_words("w1w", w1_words, N)
         w1s = load_scales("w1s", w1_scales, N, nc.sync)
         n3_l = load_list("n3_l", n3)

from contextlib import ExitStack

import concourse.mybir as mybir
from concourse.masks import make_identity

F32 = mybir.dt.float32
BF16 = mybir.dt.bfloat16
I32 = mybir.dt.int32
U32 = mybir.dt.uint32
U16 = mybir.dt.uint16
U8 = mybir.dt.uint8
FP8X4 = mybir.dt.float8_e4m3fn_x4
ALU = mybir.AluOpType
ACT = mybir.ActivationFunctionType

P = 128
PACK = 4
T = 2048
N = 512
WIDE = 2 * N
FLOPS = 3 * 2 * 512 * 512 * 512
OUT_CHUNKS = ((0, 256), (256, 128), (384, 128))


def tile_picked_kqmedhopdhop_none_po_kernel(tc, x_words, x_scales, w1_words, w1_scales, w2_words, w2_scales, ga, gb,
        offs, two, n1, n2, n3, n4, n5, n6, out_0, out_1, out_2):
    nc = tc.nc
    with ExitStack() as ctx:
        lists = ctx.enter_context(tc.tile_pool(name="lists", bufs=1))
        sb = ctx.enter_context(tc.tile_pool(name="sb", bufs=1))
        psum = ctx.enter_context(tc.psum_pool(name="psum", bufs=1))

        def tile(name, shape, dtype):
            return sb.tile(shape, dtype, name=name, align_bytes=64)

        def load_list(name, src):
            held = lists.tile([P, N // 16], U16, name=name)
            nc.sync.dma_start(held[:], src)
            return held

        def load_words(name, src, width):
            held = tile(name, [P, width], I32)
            nc.sync.dma_start(held[:], src[0].rearrange("p n t -> p (n t)").bitcast(I32))
            return held

        def load_scales(name, src, width, queue):
            held = tile(name, [P, width], U8)
            nc.vector.memset(held[:].bitcast(I32), 0)
            for q in range(4):
                queue.dma_start(held[32 * q : 32 * q + 4, :].bitcast(I32), src[0, 4 * q : 4 * q + 4, :].bitcast(I32))
            return held

        two_l = load_list("two_l", two)
        xw = load_words("xw", x_words, T)
        xs = load_scales("xs", x_scales, T, nc.sync)
        w2w = load_words("w2w", w2_words, N)
        offs_l = load_list("offs_l", offs)
        w2s = load_scales("w2s", w2_scales, N, nc.scalar)
        w1w = load_words("w1w", w1_words, N)
        w1s = load_scales("w1s", w1_scales, N, nc.sync)
        n3_l = load_list("n3_l", n3)

        gain_rows = tile("gain_rows", [P, P], F32)
        nc.vector.memset(gain_rows[:], 0.0)
        for r, gain in enumerate((ga, gb)):
            nc.sync.dma_start(gain_rows[PACK * r : PACK * (r + 1), :].rearrange("t (b j) -> t b j", j=8),
                                gain.rearrange("(b t j) o -> t b (j o)", t=PACK, j=8))
        ident = tile("ident", [P, P], F32)
        make_identity(nc, ident[:])
        n1_l = load_list("n1_l", n1)
        n2_l = load_list("n2_l", n2)
        n4_l = load_list("n4_l", n4)
        n5_l = load_list("n5_l", n5)
        n6_l = load_list("n6_l", n6)

        def pick_scales(name, picks):
            got = tile(name, [P, N], U8)
            nc.vector.tensor_copy(got[:], xs[:].indirect(picks[:]))
            return got

        def pick_words(name, picks):
            got = tile(name, [P, N], I32)
            nc.vector.tensor_copy(got[:].bitcast(U32), xw[:].bitcast(U32).indirect(picks[:]))
            return got

        def deal(name, src, dtype):
            dealt = tile(name, [P, N], dtype)
            nc.vector.tensor_copy(dealt[:].bitcast(I32).rearrange("p (t b j) -> p b t j", t=PACK, b=16),
                                  src[:].bitcast(I32).rearrange("p (b t j) -> p b t j", t=PACK, b=16))
            return dealt

        def product(tag, t, lw, ls, rw, rs):
            bank = psum.tile([P, N], F32, name=f"{tag}{t}", tag=f"{tag}{t}")
            nc.tensor.matmul_mx(out=bank[:], lhsT=lw.bitcast(FP8X4), lhsT_scale=ls, rhs=rw.bitcast(FP8X4), rhs_scale=rs, start=True, stop=True)
            return bank

        xs_two = pick_scales("xs_two", two_l)
        xw_two = pick_words("xw_two", two_l)
        w2wd = deal("w2wd", w2w, I32)
        w2sd = deal("w2sd", w2s, U8)
        xs_offs = pick_scales("xs_offs", offs_l)
        xw_offs = pick_words("xw_offs", offs_l)
        w1wd = deal("w1wd", w1w, I32)
        w1sd = deal("w1sd", w1s, U8)

        b_plain = tile("b_plain", [P, PACK, N], F32)
        st_win = []
        for t in range(PACK):
            bank = product("pb", t, w2wd[:, P * t : P * (t + 1)], w2sd[:, P * t : P * (t + 1)], xw_two[:], xs_two[:])
            b_win = tile(f"b_win{t}", [P, WIDE], F32)
            nc.scalar.copy(b_win[:, 0:N], bank[:])
            nc.scalar.copy(b_plain[:, t, :], bank[:])
            st = tile(f"st_win{t}", [P, WIDE], F32)
            nc.vector.tensor_tensor(st[:, 0:N], b_win[:].indirect(n3_l[:]), b_plain[:, t, :], ALU.subtract)
            st_win.append(st)

        gain_bank = psum.tile([P, P], F32, name="gain_bank", tag="pa3")
        nc.tensor.transpose(gain_bank[:], gain_rows[:], ident[:])
        gains = tile("gains", [P, 2 * PACK], F32)
        nc.scalar.copy(gains[:], gain_bank[:, 0 : 2 * PACK])

        a_win = []
        a_plain = tile("a_plain", [P, PACK, N], F32)
        for t in range(PACK):
            bank = product("pa", t, w1wd[:, P * t : P * (t + 1)], w1sd[:, P * t : P * (t + 1)], xw_offs[:], xs_offs[:])
            win = tile(f"a_win{t}", [P, WIDE], F32)
            nc.scalar.activation(win[:, 0:N], bank[:], ACT.Copy, scale=gains[:, t : t + 1])
            nc.scalar.activation(a_plain[:, t, :], bank[:], ACT.Copy, scale=gains[:, t : t + 1])
            a_win.append(win)

        z2 = tile("z2", [P, PACK, N], F32)
        for t in range(PACK):
            nc.scalar.activation(z2[:, t, :], st_win[t][:].indirect(n4_l[:]), ACT.Sigmoid)

        d1 = tile("d1", [P, PACK, N], F32)
        d2 = tile("d2", [P, PACK, N], F32)
        for t in range(PACK):
            nc.vector.tensor_tensor(d1[:, t, :], a_win[t][:].indirect(n1_l[:]), a_plain[:, t, :], ALU.subtract)
            nc.vector.tensor_tensor(d2[:, t, :], a_win[t][:].indirect(n2_l[:]), a_plain[:, t, :], ALU.subtract)

        b_gain = tile("b_gain", [P, PACK, N], F32)
        for t in range(PACK):
            nc.scalar.activation(b_gain[:, t, :], b_plain[:, t, :], ACT.Copy, scale=gains[:, PACK + t : PACK + t + 1])

        zb = tile("zb", [P, N * PACK], BF16)
        zb_pairs = zb[:].bitcast(F32).rearrange("p (u m w) -> p u m w", u=PACK, w=2)

        turned = [psum.tile([P, PACK, P], F32, name=f"turned{h}", tag=f"pa{h}") for h in range(3)]
        for h in range(3):
            for t in range(PACK):
                nc.tensor.matmul(turned[h][:, t, :], a_plain[:, t, P * h : P * (h + 1)], ident[:], start=(t == 0), stop=False, is_transpose=True)

        def upper_clamp(h):
            cols = slice(P * h, P * (h + 1))
            nc.vector.scalar_tensor_tensor(d2[:, :, cols], d1[:, :, cols], 0.0, d2[:, :, cols], ALU.max, ALU.min)

        def finish_z(h):
            cols = slice(P * h, P * (h + 1))
            nc.vector.scalar_tensor_tensor(d2[:, :, cols], d1[:, :, cols], 0.0, d2[:, :, cols], ALU.min, ALU.max)
            if h == 3:
                nc.vector.tensor_tensor(zb[:].rearrange("p (u m t) -> p m t u", u=PACK, t=PACK)[:, 32 * h : 32 * (h + 1), :, :],
                                        a_plain[:, :, cols].rearrange("p t (m u) -> p m t u", u=PACK),
                                        d2[:, :, cols].rearrange("p t (m u) -> p m t u", u=PACK), ALU.add)
                return None
            for t in range(PACK):
                nc.tensor.matmul(turned[h][:, t, :], d2[:, t, cols], ident[:], start=False, stop=(t == PACK - 1), is_transpose=True)
            zt = tile(f"zt{h}", [P, N], BF16)
            nc.scalar.copy(zt[:].rearrange("c (w p e) -> c w p e", w=2, e=2), turned[h][:].rearrange("c (w e) p -> c w p e", e=2))
            return zt

        def turn_back(h, zt):
            back = psum.tile([P, 2, P], F32, name=f"back{h}", tag=f"pa{h + 1}")
            for w in range(2):
                nc.tensor.transpose(back[:, w, :], zt[:].bitcast(F32)[:, P * w : P * (w + 1)], ident[:])
            nc.scalar.copy(zb_pairs[:, :, 32 * h : 32 * (h + 1), :], back[:].rearrange("p w (m u) -> p u m w", u=PACK))

        zts = []
        upper_clamp(0)
        for h in range(4):
            if h < 3:
                upper_clamp(h + 1)
            zts.append(finish_z(h))
            if h > 0:
                turn_back(h - 1, zts[h - 1])

        z2b = tile("z2b", [P, N, PACK], BF16)
        z2w = tile("z2w", [P, N], I32)
        z2s = tile("z2s", [P, N], U8)
        halves = (slice(0, N // 2), slice(N // 2, N))
        for cols in halves:
            nc.vector.tensor_tensor(z2b[:, cols, :].rearrange("p (c i) t -> p c t i", i=4),
                                    b_gain[:, :, cols].rearrange("p t (c i) -> p c t i", i=4),
                                    z2[:, :, cols].rearrange("p t (c i) -> p c t i", i=4), ALU.mult)
        for cols in halves:
            nc.vector.quantize_mx(out=z2w[:, cols].bitcast(FP8X4), scales=z2s[:, cols], in_=z2b[:, cols, :].rearrange("p c t -> p (c t)"))

        st2_win = []
        st2_plain = tile("st2_plain", [P, PACK, N], F32)
        s_plain = tile("s_plain", [P, PACK, N], F32)
        s_win = [tile(f"s_win{u}", [P, WIDE], F32) for u in range(PACK)]
        zq = []
        for u in range(PACK):
            zw = tile(f"zw{u}", [P, P], I32)
            zs = tile(f"zs{u}", [P, P], U8)
            nc.vector.quantize_mx(out=zw[:].bitcast(FP8X4), scales=zs[:], in_=zb[:, N * u : N * (u + 1)])
            zq.append((zw, zs))
        first = []
        for tag, cols in zip(("pa0", "pb0"), halves):
            bank = psum.tile([P, N // 2], F32, name=f"first_{tag}", tag=tag)
            nc.tensor.matmul_mx(out=bank[:], lhsT=zq[0][0][:].bitcast(FP8X4), lhsT_scale=zq[0][1][:],
                                rhs=z2w[:, cols].bitcast(FP8X4), rhs_scale=z2s[:, cols], start=True, stop=True)
            first.append(bank)
        banks = [product("pb", u, zq[u][0][:], zq[u][1][:], z2w[:], z2s[:]) for u in range(1, PACK)]
        nc.scalar.activation(s_win[0][:, halves[0]], first[0][:], ACT.Copy, scale=-1.0 / 32.0)
        nc.vector.tensor_scalar(s_win[0][:, halves[1]], first[1][:], -1.0 / 32.0, None, ALU.mult)
        nc.vector.tensor_scalar(s_plain[:, 0, :], s_win[0][:, 0:N], 2.0, None, ALU.mult)
        for u in range(PACK):
            if u > 0:
                nc.scalar.activation(s_win[u][:, 0:N], banks[u - 1][:], ACT.Copy, scale=-1.0 / 32.0)
                nc.scalar.activation(s_plain[:, u, :], banks[u - 1][:], ACT.Copy, scale=-1.0 / 16.0)
            st2 = tile(f"st2_win{u}", [P, N], F32)
            nc.vector.tensor_tensor(st2[:], s_win[u][:].indirect(n5_l[:]), s_plain[:, u, :], ALU.add)
            st2_win.append(st2)
        for u in range(PACK):
            nc.scalar.copy(st2_plain[:, u, :], st2_win[u][:])

        rows = out_0.rearrange("(p t) v -> p t v", t=PACK)
        words_out = out_1[0].rearrange("p c r -> p (c r)").bitcast(I32)
        os_t = tile("os_t", [P, N], U8)
        for h, (c0, width) in enumerate(OUT_CHUNKS):
            cols = slice(c0, c0 + width)
            y = tile(f"y{h}", [P, PACK, width], F32)
            for u in range(PACK):
                nc.vector.tensor_tensor(y[:, u, :], st2_win[u][:].indirect(n6_l[:, c0 // 16 : (c0 + width) // 16]),
                                        st2_plain[:, u, cols], ALU.subtract)
            nc.sync.dma_start(rows[:, :, cols], y[:])
            yb = tile(f"yb{h}", [P, width, PACK], BF16)
            rounding_copy = nc.vector.tensor_copy if h == len(OUT_CHUNKS) - 1 else nc.scalar.copy
            rounding_copy(yb[:].rearrange("p (c i) t -> p c t i", i=4), y[:].rearrange("p t (c i) -> p c t i", i=4))
            yw = tile(f"yw{h}", [P, width], I32)
            nc.vector.quantize_mx(out=yw[:].bitcast(FP8X4), scales=os_t[:, cols], in_=yb[:].rearrange("p c t -> p (c t)"))
            nc.sync.dma_start(words_out[:, cols], yw[:])
        for q in range(4):
            queue = nc.scalar if q % 2 else nc.sync
            queue.dma_start(out_2[0, 4 * q : 4 * q + 4, :].bitcast(I32), os_t[32 * q : 32 * q + 4, :].bitcast(I32))
